import numpy as np
import ml_dtypes


def mxq(x, axis, fmt="e4m3"):
    dtype, down = {"e4m3": (ml_dtypes.float8_e4m3fn, 7), "e5m2": (ml_dtypes.float8_e5m2, 14)}[fmt]
    v = np.moveaxis(np.asarray(x, np.float32).astype(ml_dtypes.bfloat16).astype(np.float64), axis, -1)
    blocks = v.reshape(v.shape[:-1] + (-1, 32))
    amax = np.abs(blocks).max(-1, keepdims=True)
    byte = np.maximum(np.where(amax > 0, np.frexp(amax)[1] - 1 + 127, 0) - down, 1)
    scale = np.exp2(byte - 127.0)
    codes = (blocks / scale).astype(np.float32).astype(dtype).astype(np.float64)
    return np.moveaxis((codes * scale).reshape(v.shape), -1, axis)


WIDE = False


def mx_kscale(k):
    if not WIDE:
        return np.ones(k)
    levels = np.array([10, -10, 5, -5, 0])
    if k % 512:
        return np.exp2(np.random.permutation(np.resize(levels, k // 32))).repeat(32)
    a = np.empty((k // 512, 16))
    for p in range(k // 512):
        a[p, :8] = np.random.permutation(np.resize(levels, 8))
        for g in range(8):
            far = levels[np.abs(levels - a[p, g]) >= 10]
            a[p, g + 8] = far[np.random.randint(len(far))]
    return np.exp2(a.ravel()).repeat(32)


def f64(x):
    return np.asarray(x).astype(np.float64)


def striped(idx):
    return np.tile(idx.reshape(-1, 16).T, (8, 1)).astype(np.uint16)


def unstriped(offs):
    return offs[:16].T.reshape(-1).astype(np.int64)


E2M1 = np.array([0.0, 0.5, 1.0, 1.5, 2.0, 3.0, 4.0, 6.0, -0.0, -0.5, -1.0, -1.5, -2.0, -3.0, -4.0, -6.0])


def pack_weight(w, fmt):
    k, n = w.shape
    w = f64(np.asarray(w, np.float32).astype(ml_dtypes.bfloat16)).reshape(k // 32, 32, n)
    amax = np.abs(w).max(1)
    if fmt == "e4m3":
        byte = np.frexp(amax)[1] - 1 + 127 - 7
    else:
        mant, ex = np.frexp(amax / 6.0)
        byte = np.where(mant > 0.5, ex, ex - 1) + 127
    byte = np.clip(np.where(amax > 0, byte, 1), 1, 254)
    scaled = (w * np.exp2(127.0 - byte)[:, None, :]).reshape(k, n).astype(np.float32)
    by_word = np.ascontiguousarray(scaled.reshape(k // 512, 128, 4, n).transpose(0, 1, 3, 2))
    if fmt == "e4m3":
        words = by_word.astype(ml_dtypes.float8_e4m3fn).view(np.uint8)
    else:
        c = by_word.astype(ml_dtypes.float4_e2m1fn).view(np.uint8) & 0xF
        words = (c[..., 0::2] | (c[..., 1::2] << 4)).reshape(k // 512, 128, 2 * n)
    return np.ascontiguousarray(words), np.ascontiguousarray(byte.astype(np.uint8).reshape(k // 512, 16, n))


def unpack_weight(words, scales, fmt):
    g, _, n = scales.shape
    words = np.ascontiguousarray(words).reshape(g, 128, n, -1)
    if fmt == "e4m3":
        vals = words.view(ml_dtypes.float8_e4m3fn).astype(np.float64)
    else:
        nib = np.empty((g, 128, n, 4), np.uint8)
        nib[..., 0::2] = words & 0xF
        nib[..., 1::2] = words >> 4
        vals = E2M1[nib]
    vals = vals * np.repeat(np.exp2(scales.astype(np.float64) - 127.0), 8, axis=1)[..., None]
    return vals.transpose(0, 1, 3, 2).reshape(g * 512, n)


def gelu(v):
    return 0.5 * v * (1.0 + np.tanh(np.sqrt(2.0 / np.pi) * (v + 0.044715 * v**3)))


K, H, N, T, T2, S, P = 1024, 1024, 512, 2048, 2048, 512, 1024

def setup_inputs():
    n = np.random.standard_normal
    s = mx_kscale(K)[:, None]
    u = mx_kscale(H)[:, None]
    perm = np.random.permutation(T2)
    d = {}
    d["tab_words"], d["tab_scales"] = pack_weight(n((K, T)) * s, "e4m3")
    d["tab2_words"], d["tab2_scales"] = pack_weight(n((K, T)) * s, "e4m3")
    d["offs"] = striped(np.random.permutation(T)[:S])
    d["offs2"] = striped(np.random.permutation(T)[:S])
    d["offs3"] = striped(perm[:S])
    d["offs4"] = striped(perm[S:2 * S])
    d["offs5"] = striped(np.random.permutation(T2)[:P])
    d["w1"] = (1.3 * n((K, H)) / K**0.5 / s).astype(np.float32)
    d["base"] = (0.8 * n(H)).astype(np.float32)
    d["wg1"] = np.exp(0.3 * n((128, S))).astype(np.float32)
    d["wg2"] = np.exp(0.3 * n((128, S))).astype(np.float32)
    d["page0"] = (1.3 * n((H, T2))).astype(np.float32)
    d["gain"] = (np.exp(0.3 * n(H)) * u[:, 0]).astype(np.float32)
    d["w2"] = (1.6 * n((H, N)) / H**0.5 / u).astype(np.float32)
    d["w4_words"], d["w4_scales"] = pack_weight(3.5 * n((H, N)) / H**0.5 / u, "e2m1")
    return d

def reference(tab_words, tab_scales, tab2_words, tab2_scales, offs, offs2, offs3, offs4, offs5,
              w1, base, wg1, wg2, page0, gain, w2, w4_words, w4_scales):
    v = unpack_weight(tab_words, tab_scales, "e4m3")[:, unstriped(offs)]
    v2 = unpack_weight(tab2_words, tab2_scales, "e4m3")[:, unstriped(offs2)]
    wq = mxq(f64(w1), 0, "e4m3")
    h1 = (wq.T @ v) - f64(base)[:, None]
    h2 = np.abs(wq.T @ v2)
    page = f64(page0).copy()
    page[:, unstriped(offs3)] = np.tile(f64(wg1), (H // 128, 1)) * h1
    page[:, unstriped(offs4)] = np.tile(f64(wg2), (H // 128, 1)) * h2
    x = np.tanh(page[:, unstriped(offs5)]) * f64(gain)[:, None]
    xq = mxq(x, 0, "e4m3")
    y1 = mxq(f64(w2), 0, "e4m3").T @ xq
    y2 = unpack_weight(w4_words, w4_scales, "e2m1").T @ xq
    return np.maximum(y1, 1.0 / (1.0 + np.exp(-y2)))

from contextlib import ExitStack

import concourse.mybir as mybir
from concourse.masks import make_identity

K, H, N, T, S, R = 1024, 1024, 512, 2048, 512, 1024
FLOPS = 2 * K * H * S * 2 + 2 * H * N * R * 2

F32 = mybir.dt.float32
BF16 = mybir.dt.bfloat16
I32 = mybir.dt.int32
U32 = mybir.dt.uint32
U16 = mybir.dt.uint16
U8 = mybir.dt.uint8
FP8X4 = mybir.dt.float8_e4m3fn_x4
FP4X4 = mybir.dt.float4_e2m1fn_x4
ACT = mybir.ActivationFunctionType
ALU = mybir.AluOpType

P = 128
PACK = 4
KP = P * PACK
BANK = 512
LAST = 256
Y2_BANKS = ((0, 1, 2, 3), (0, 2, 3, 6))
Y1_BANKS = ((4, 5, 6, 7), (1, 4, 5, 7))


def tile_list_cork_taint_page_kernel(
    tc, tab_words, tab_scales, tab2_words, tab2_scales, offs, offs2, offs3, offs4, offs5,
    w1, base, wg1, wg2, page0, gain, w2, w4_words, w4_scales, out,
):
    nc = tc.nc
    with ExitStack() as ctx:
        lists = ctx.enter_context(tc.tile_pool(name="lists", bufs=1))
        keep = ctx.enter_context(tc.tile_pool(name="keep", bufs=1))
        slots = ctx.enter_context(tc.tile_pool(name="slots", bufs=1))
        ring = ctx.enter_context(tc.tile_pool(name="ring", bufs=2))
        psum = ctx.enter_context(tc.psum_pool(name="psum", bufs=1))

        def load_list(src, name):
            t = lists.tile(list(src.shape), U16, name=name)
            nc.sync.dma_start(t[:], src)
            return t

        def slot(i, shape, dtype, name):
            return slots.tile(shape, dtype, name=name, tag="slot%d" % i, align_bytes=64)

        banks_used = [0]

        def next_bank(shape, name):
            i = banks_used[0] % 8
            banks_used[0] = banks_used[0] + 1
            return psum.tile(shape, F32, name=name, tag="bank%d" % i)

        def load_rows(src, i, name):
            raw = slot(i, [P, PACK, KP], F32, name)
            nc.sync.dma_start(raw[:], src.rearrange("(p j) c -> p j c", j=PACK))
            return raw

        def load_w1_slice(s):
            raw = slots.tile([P, 2, PACK, P], F32, name="raw_s%d" % s, tag="half%d" % s, align_bytes=64)
            for a in range(2):
                src = w1[KP * a : KP * (a + 1), P * s : P * (s + 1)]
                nc.sync.dma_start(raw[:, a], src.rearrange("(p j) c -> p j c", j=PACK))
            return raw

        def load_words(src, a, i, name):
            t = slot(i, [P, T], U32, name)
            nc.sync.dma_start(t[:].bitcast(I32), src[a].rearrange("p t i -> p (t i)").bitcast(I32))
            return t

        def zero_plane(shape, name):
            t = keep.tile(shape, U8, name=name, align_bytes=64)
            nc.vector.memset(t[:].bitcast(I32), 0)
            return t

        def load_table_scales(queue, t, src):
            for q in range(4):
                queue.dma_start(
                    t[32 * q : 32 * q + 8, :].bitcast(I32),
                    src[:, 4 * q : 4 * q + 4, :].bitcast(I32),
                )

        def load_plain(src, name):
            t = keep.tile(list(src.shape), F32, name=name)
            nc.sync.dma_start(t[:], src)
            return t

        def load_dealt_gates(src, name):
            t = keep.tile([P, PACK, S], F32, name=name)
            rows = src.rearrange("(q t) j -> q t j", t=PACK)
            for q in range(4):
                nc.sync.dma_start(t[32 * q : 32 * q + 32], rows)
            return t

        def page_rows(s):
            if s < PACK:
                return page0[P * s : P * (s + 1), :]
            return page0[KP:H, :].rearrange("(p t) c -> p t c", t=PACK)[:, s - PACK, :]

        pages = [keep.tile([P, T], F32, name="page%d" % s) for s in range(8)]

        def load_page(s):
            nc.sync.dma_start(pages[s][:], page_rows(s))

        def load_page_pair(s):
            for cols in (slice(0, T - LAST), slice(T - LAST, T)):
                for u in (s, s + 1):
                    nc.sync.dma_start(pages[u][:, cols], page_rows(u)[:, cols])

        def load_vec(src, name):
            lo = keep.tile([P, PACK], F32, name=name + "_lo")
            with nc.allow_non_contiguous_dma(reason="one value a partition"):
                nc.sync.dma_start(lo[:], src[0:KP].rearrange("(s p) -> p s", p=P))
            return lo

        def load_vec_hi(src, name):
            hi = keep.tile([P, PACK], F32, name=name + "_hi")
            nc.sync.dma_start(hi[:], src[KP:H].rearrange("(p t) -> p t", t=PACK))
            return hi

        def cell(i, dtype, name):
            return slots.tile([P, S], dtype, name=name, tag="cell%d" % i, align_bytes=64)

        def quantize(grouped, name, where=None):
            cols = grouped.shape[1] // PACK
            if where is None:
                codes = keep.tile([P, cols], U32, name=name + "_codes", align_bytes=64)
            elif not isinstance(where, int):
                codes = where
            else:
                codes = cell(where, U32, name + "_codes")
            scales = keep.tile([P, cols], U8, name=name + "_scales", align_bytes=64)
            nc.vector.quantize_mx(out=codes[:].bitcast(FP8X4), scales=scales[:], in_=grouped)
            return codes, scales

        def cast_w1_slice(raw, copy, name):
            grouped = ring.tile([P, 2 * P * PACK], BF16, name="grouped", bufs=4, align_bytes=64)
            copy(grouped[:].rearrange("p (a c i j) -> p a c j i", a=2, i=4, j=PACK),
                 raw[:].rearrange("p a j (c i) -> p a c j i", i=4))
            return quantize(grouped[:], name)

        def cast_w1_dealt(raw, name):
            grouped = ring.tile([P, KP * PACK], BF16, name="grouped", bufs=4, align_bytes=64)
            nc.scalar.copy(grouped[:].rearrange("p (t m j) -> p m j t", t=PACK, j=PACK),
                           raw[:].rearrange("p j (m t) -> p m j t", t=PACK))
            return grouped

        def cast_w2(raw, name):
            grouped = ring.tile([P, KP * PACK], BF16, name="grouped", bufs=4, align_bytes=64)
            nc.scalar.copy(grouped[:].rearrange("p (c i j) -> p c j i", i=4, j=PACK),
                           raw[:].rearrange("p j (c i) -> p c j i", i=4))
            return grouped

        def gather(window, offsets, dtype, name):
            t = keep.tile([P, S], dtype, name=name, align_bytes=64)
            nc.vector.tensor_copy(t[:], window[:].indirect(offsets[:]))
            return t

        sc1 = zero_plane([P, T], "tab_sc")
        sc2 = zero_plane([P, T], "tab2_sc")
        w4s = zero_plane([P, 2 * N], "w4_sc")
        ident = keep.tile([P, P], F32, name="ident")
        make_identity(nc, ident[:])

        o1 = load_list(offs, "o1")
        o3 = load_list(offs3, "o3")
        base_lo = load_vec(base, "base")
        tw0 = load_words(tab_words, 0, 2, "tw0")
        load_table_scales(nc.sync, sc1, tab_scales)
        warm = keep.tile([P, 1], F32, name="warm")
        nc.scalar.activation(warm[:], ident[:, 0:1], ACT.Sigmoid)
        raw_s = [load_w1_slice(0)]
        tw1 = load_words(tab_words, 1, 3, "tw1")
        g1n = load_plain(wg1, "g1n")
        load_page(0)
        o2 = load_list(offs2, "o2")
        load_table_scales(nc.sync, sc2, tab2_scales)
        raw_s.append(load_w1_slice(1))
        uw0 = load_words(tab2_words, 0, 4, "uw0")
        uw1 = load_words(tab2_words, 1, 5, "uw1")
        load_page(1)
        raw_s.append(load_w1_slice(2))
        raw_s.append(load_w1_slice(3))
        g2n = load_plain(wg2, "g2n")
        o4 = load_list(offs4, "o4")
        base_hi = load_vec_hi(base, "base")
        gain_lo = load_vec(gain, "gain")
        gain_hi = load_vec_hi(gain, "gain")
        o5 = load_list(offs5, "o5")
        raw01 = load_rows(w1[0:KP, KP:H], 6, "raw01")
        raw11 = load_rows(w1[KP:K, KP:H], 7, "raw11")
        load_page_pair(2)
        g1d = load_dealt_gates(wg1, "g1d")
        g2d = load_dealt_gates(wg2, "g2d")
        raw20 = load_rows(w2[0:KP, :], 4, "raw20")
        raw21 = load_rows(w2[KP:H, :], 5, "raw21")
        load_page_pair(4)
        w4w = keep.tile([P, 2, 2 * N], U8, name="w4w", align_bytes=64)
        nc.sync.dma_start(w4w[:].bitcast(I32), w4_words.rearrange("a p c -> p a c").bitcast(I32))
        for q in range(4):
            nc.sync.dma_start(
                w4s[32 * q : 32 * q + 4, :].rearrange("r (a n) -> r a n", a=2).bitcast(I32),
                w4_scales[:, 4 * q : 4 * q + 4, :].rearrange("a r n -> r a n").bitcast(I32),
            )
        load_page_pair(6)

        neg_lo = keep.tile([P, PACK], F32, name="neg_lo")
        nc.scalar.mul(neg_lo[:], base_lo[:], -1.0)

        ws = [cast_w1_slice(raw_s[0], nc.vector.tensor_copy, "ws0")]
        v1s = gather(sc1, o1, U8, "v1s")
        v1 = [gather(tw0, o1, U32, "v10"), gather(tw1, o1, U32, "v11")]
        wd = []
        neg = [neg_lo]

        top_cell = [0, 1, 2, 3, 0, 1, 6, 7]
        bottom_cell = [4, 5, 6, 7, 4, 5, 8, 9]
        h1 = {}
        h2 = {}

        def first_stage(v, vs, s, top):
            b, t = divmod(s, PACK)
            acc = next_bank([P, BANK], "acc")
            for a in range(2):
                if b == 0:
                    codes, scales = ws[s]
                    cols = slice(P * a, P * (a + 1))
                else:
                    codes, scales = wd[a]
                    cols = slice(P * t, P * (t + 1))
                nc.tensor.matmul_mx(
                    out=acc[:], lhsT=codes[:, cols].bitcast(FP8X4), lhsT_scale=scales[:, cols],
                    rhs=v[a][:].bitcast(FP8X4), rhs_scale=vs[4 * a : P, :],
                    start=(a == 0), stop=(a == 1),
                )
            if top:
                h1[s] = cell(top_cell[s], F32, "h1_%d" % s)
                nc.scalar.activation(h1[s][:], acc[:], ACT.Identity, bias=neg[b][:, t : t + 1])
            else:
                h2[s] = cell(bottom_cell[s], F32, "h2_%d" % s)
                nc.scalar.activation(h2[s][:], acc[:], ACT.Abs)

        def put_top(s):
            gate = g1n[:] if s < PACK else g1d[:, s - PACK, :]
            nc.vector.tensor_tensor(pages[s][:].indirect(o3[:]), h1[s][:], gate, ALU.mult)

        def put_bottom(s):
            gate = g2n[:] if s < PACK else g2d[:, s - PACK, :]
            nc.vector.tensor_tensor(pages[s][:].indirect(o4[:]), h2[s][:], gate, ALU.mult)

        xg = [slot(2, [P, R * PACK], BF16, "xg0"), slot(3, [P, R * PACK], BF16, "xg1")]
        fetched = [0]

        def fetch(s, lo, hi):
            got = slots.tile([P, hi - lo], F32, name="got", tag="half%d" % (fetched[0] % 4), align_bytes=64)
            fetched[0] = fetched[0] + 1
            nc.vector.tensor_copy(got[:], pages[s][:].indirect(o5[:, lo // 16 : hi // 16]))
            return got

        def fetch_plain(s):
            got = fetch(s, 0, R)
            nc.scalar.activation(got[:], got[:], ACT.Tanh)
            xs = ring.tile([P, R], BF16, name="xs", align_bytes=64)
            nc.scalar.activation(xs[:], got[:], ACT.Copy, scale=gain_lo[:, s : s + 1])
            acc = next_bank([P, 4, P], "turn")
            for u in range(4):
                nc.tensor.transpose(acc[:, u, :], xs[:].bitcast(F32)[:, P * u : P * (u + 1)], ident[:])
            nc.scalar.copy(turned[:, :, :, 32 * s : 32 * (s + 1)], acc[:].rearrange("w u (i t) -> w u t i", t=PACK))

        def turn_back(u):
            acc = next_bank([P, PACK, P], "back")
            for t in range(PACK):
                nc.tensor.transpose(acc[:, t, :], turned[:, u, t, :], ident[:])
            dst = xg[0][:, 2 * P * PACK * u : 2 * P * PACK * (u + 1)].rearrange("p (c t) -> p c t", t=PACK)
            nc.scalar.copy(dst, acc[:].bitcast(BF16).rearrange("p t c -> p c t"))

        def fetch_dealt(s, lo, hi):
            t = s - PACK
            got = fetch(s, lo, hi)
            dst = xg[1][:].rearrange("p (c j) -> p c j", j=PACK)[:, lo:hi, t]
            half = (hi - lo) // 2
            parts = (slice(0, half), slice(half, hi - lo))
            for part in parts:
                nc.scalar.activation(got[:, part], got[:, part], ACT.Tanh)
            for part in parts:
                nc.scalar.activation(dst[:, part], got[:, part], ACT.Copy, scale=gain_hi[:, t : t + 1])

        xq = {}

        def quantize_x(b, c, where):
            xq[b, c] = quantize(xg[b][:, BANK * PACK * c : BANK * PACK * (c + 1)], "x%d%d" % (b, c), where)

        first_stage(v1, v1s, 0, True)
        put_top(0)
        v2s = gather(sc2, o2, U8, "v2s")
        ws.append(cast_w1_slice(raw_s[1], nc.scalar.copy, "ws1"))
        v2 = [gather(uw0, o2, U32, "v20"), gather(uw1, o2, U32, "v21")]
        first_stage(v1, v1s, 1, True)
        first_stage(v2, v2s, 0, False)
        first_stage(v2, v2s, 1, False)
        for s in (2, 3):
            ws.append(cast_w1_slice(raw_s[s], nc.scalar.copy, "ws%d" % s))
            first_stage(v1, v1s, s, True)
        for s in (2, 3):
            first_stage(v2, v2s, s, False)
        put_top(1)
        put_bottom(0)
        put_bottom(1)

        neg_hi = keep.tile([P, PACK], F32, name="neg_hi")
        nc.scalar.mul(neg_hi[:], base_hi[:], -1.0)
        neg.append(neg_hi)
        w1_hi = [cast_w1_dealt(raw01, "w01"), cast_w1_dealt(raw11, "w11")]
        turned = keep.tile([P, 4, PACK, P], F32, name="turned")
        fetch_plain(0)
        fetch_plain(1)
        put_top(2)
        put_top(3)
        put_bottom(2)
        wd.append(quantize(w1_hi[0][:], "w01", 2))
        put_bottom(3)
        wd.append(quantize(w1_hi[1][:], "w11", 3))
        for s in (4, 6):
            first_stage(v1, v1s, s, True)
            first_stage(v1, v1s, s + 1, True)
            first_stage(v2, v2s, s, False)
            first_stage(v2, v2s, s + 1, False)
        fetch_plain(2)
        fetch_plain(3)
        for u in range(4):
            turn_back(u)
        w2_grouped = [cast_w2(raw20, "w20"), cast_w2(raw21, "w21")]
        put_top(4)
        put_top(5)
        put_bottom(4)
        put_bottom(5)
        fetch_dealt(4, 0, R)
        fetch_dealt(5, 0, R)
        w2q = {1: quantize(w2_grouped[1][:], "w21", 1)}
        put_top(6)
        put_top(7)
        put_bottom(6)
        quantize_x(0, 0, 7)
        fetch_dealt(6, 0, R)
        put_bottom(7)

        accs = {}
        floor = slot(6, [P, 4, BANK], F32, "floor")
        res = [slot(7, [P, 4, BANK], F32, "res0"), slot(5, [P, 4, BANK], F32, "res1")]

        def floor_pass(b, c, n):
            codes, scales = xq[b, c]
            if b == 0:
                accs[2, c, n] = psum.tile([P, BANK], F32, name="y2", tag="bank%d" % Y2_BANKS[c][n])
            nc.tensor.matmul_mx(
                out=accs[2, c, n][:], lhsT=w4w[:, b, 2 * P * n : 2 * P * (n + 1)].bitcast(FP4X4),
                lhsT_scale=w4s[:, N * b + P * n : N * b + P * (n + 1)],
                rhs=codes[:].bitcast(FP8X4), rhs_scale=scales[:], start=(b == 0), stop=(b == 1),
            )

        def main_pass(b, c, n):
            codes, scales = xq[b, c]
            if b == 0:
                accs[1, c, n] = psum.tile([P, BANK], F32, name="y1", tag="bank%d" % Y1_BANKS[c][n])
            wc, wsc = w2q[b]
            nc.tensor.matmul_mx(
                out=accs[1, c, n][:], lhsT=wc[:, P * n : P * (n + 1)].bitcast(FP8X4), lhsT_scale=wsc[:, P * n : P * (n + 1)],
                rhs=codes[:].bitcast(FP8X4), rhs_scale=scales[:], start=(b == 0), stop=(b == 1),
            )

        def finish(c, n):
            nc.scalar.activation(floor[:, n, :], accs[2, c, n][:], ACT.Sigmoid)
            nc.vector.tensor_tensor(res[c][:, n, :], accs[1, c, n][:], floor[:, n, :], ALU.max)
            nc.sync.dma_start(out[P * n : P * (n + 1), BANK * c : BANK * (c + 1)], res[c][:, n, :])

        for n in range(4):
            floor_pass(0, 0, n)
        fetch_dealt(7, 0, BANK)
        late = slots.tile([P, 2, S], U32, name="late", tag="cell9", align_bytes=64)
        w2q[0] = quantize(w2_grouped[0][:], "w20", late[:, 0, :])
        for n in range(4):
            main_pass(0, 0, n)
        fetch_dealt(7, BANK, R)
        quantize_x(1, 0, 4)
        quantize_x(0, 1, late[:, 1, :])
        quantize_x(1, 1, 5)
        for n in range(4):
            floor_pass(1, 0, n)
            main_pass(1, 0, n)
            finish(0, n)
        for n in range(4):
            floor_pass(0, 1, n)
            floor_pass(1, 1, n)
            main_pass(0, 1, n)
            main_pass(1, 1, n)
            finish(1, n)
